import numpy as np
import ml_dtypes


def mxq(x, axis, fmt="e4m3"):
    dtype, down = {"e4m3": (ml_dtypes.float8_e4m3fn, 7), "e5m2": (ml_dtypes.float8_e5m2, 14)}[fmt]
    v = np.moveaxis(np.asarray(x, np.float32).astype(ml_dtypes.bfloat16).astype(np.float64), axis, -1)
    blocks = v.reshape(v.shape[:-1] + (-1, 32))
    amax = np.abs(blocks).max(-1, keepdims=True)
    byte = np.maximum(np.where(amax > 0, np.frexp(amax)[1] - 1 + 127, 0) - down, 1)
    scale = np.exp2(byte - 127.0)
    codes = (blocks / scale).astype(np.float32).astype(dtype).astype(np.float64)
    return np.moveaxis((codes * scale).reshape(v.shape), -1, axis)


WIDE = False


def mx_kscale(k):
    if not WIDE:
        return np.ones(k)
    levels = np.array([10, -10, 5, -5, 0])
    if k % 512:
        return np.exp2(np.random.permutation(np.resize(levels, k // 32))).repeat(32)
    a = np.empty((k // 512, 16))
    for p in range(k // 512):
        a[p, :8] = np.random.permutation(np.resize(levels, 8))
        for g in range(8):
            far = levels[np.abs(levels - a[p, g]) >= 10]
            a[p, g + 8] = far[np.random.randint(len(far))]
    return np.exp2(a.ravel()).repeat(32)


def f64(x):
    return np.asarray(x).astype(np.float64)


def striped(idx):
    return np.tile(idx.reshape(-1, 16).T, (8, 1)).astype(np.uint16)


def unstriped(offs):
    return offs[:16].T.reshape(-1).astype(np.int64)


def striped8(idx):
    return np.concatenate([x.reshape(-1, 16).T for x in idx]).astype(np.uint16)


def runs(offs, k):
    lists = np.stack([offs[16 * r : 16 * r + 16].T.reshape(-1) for r in range(8)]).astype(np.int64)
    return lists[np.arange(k) % 512 // 64]


def pack_weight(w):
    k, n = w.shape
    w = f64(np.asarray(w, np.float32).astype(ml_dtypes.bfloat16)).reshape(k // 32, 32, n)
    amax = np.abs(w).max(1)
    byte = np.clip(np.where(amax > 0, np.frexp(amax)[1] - 1 + 127 - 7, 1), 1, 254)
    scaled = (w * np.exp2(127.0 - byte)[:, None, :]).reshape(k, n).astype(np.float32)
    words = np.ascontiguousarray(scaled.reshape(k // 512, 128, 4, n).transpose(0, 1, 3, 2)).astype(ml_dtypes.float8_e4m3fn).view(np.uint8)
    return words, np.ascontiguousarray(byte.astype(np.uint8).reshape(k // 512, 16, n))


def unpack_weight(words, scales):
    g, p, n, _ = words.shape
    vals = np.ascontiguousarray(words).view(ml_dtypes.float8_e4m3fn).astype(np.float64) * np.repeat(np.exp2(scales.astype(np.float64) - 127.0), 8, axis=1)[..., None]
    return vals.transpose(0, 1, 3, 2).reshape(g * 512, n)

def planes(y):
    n, m = y.shape
    v = y.astype(np.float32).astype(ml_dtypes.bfloat16).astype(np.float64).reshape(n // 32, 32, m)
    top = np.abs(v).max(1)
    byte = np.clip(np.where(top > 0, np.frexp(top)[1] - 1 + 127 - 7, 1), 1, 254)
    codes = (v * np.exp2(127.0 - byte)[:, None, :]).reshape(n, m).astype(np.float32).astype(ml_dtypes.float8_e4m3fn).view(np.uint8)
    words = codes.reshape(n // 512, 128, 4, m).transpose(0, 1, 3, 2)
    return np.ascontiguousarray(words), np.ascontiguousarray(byte.astype(np.uint8).reshape(n // 512, 16, m))


K, T, S, N, H = 512, 2048, 512, 512, 512


def setup_inputs():
    n = np.random.standard_normal
    s = mx_kscale(K)[:, None]
    u = mx_kscale(H)
    packed_xT = pack_weight(n((K, T)) * s)
    packed_w1 = pack_weight(n((K, H)) / np.sqrt(K) / s)
    packed_w2 = pack_weight(n((K, H)) / np.sqrt(K) / s)
    packed_w3 = pack_weight(n((H, N)) / np.sqrt(H) / u[:, None])
    return {
        "x_words": packed_xT[0],
        "x_scales": packed_xT[1],
        "w1_words": packed_w1[0],
        "w1_scales": packed_w1[1],
        "w2_words": packed_w2[0],
        "w2_scales": packed_w2[1],
        "gn": (np.random.uniform(0.5, 1.5, (H, 1)) * u[:, None]).astype(np.float32),
        "w3_words": packed_w3[0],
        "w3_scales": packed_w3[1],
        "offs": striped(np.random.permutation(T)[:S]),
        "p1": striped8(np.stack([np.random.permutation(S) for _ in range(8)])),
        "r1": striped8(np.stack([np.random.permutation(S) for _ in range(8)])),
        "p2": striped8(np.stack([np.random.permutation(S) for _ in range(8)])),
        "r2": striped8(np.stack([np.random.permutation(S) for _ in range(8)])),
    }


def reference(x_words, x_scales, w1_words, w1_scales, w2_words, w2_scales, gn, w3_words, w3_scales, offs, p1, r1, p2, r2):
    xq = unpack_weight(x_words, x_scales)[:, unstriped(offs)]
    y = unpack_weight(w1_words, w1_scales).T @ xq
    e = unpack_weight(w2_words, w2_scales).T @ xq
    z = f64(gn) * (y + np.clip(y[np.arange(H)[:, None], runs(p1, H)] - (e[np.arange(H)[:, None], runs(r1, H)]), -0.75, 0.75) + np.clip(y[np.arange(H)[:, None], runs(p2, H)] - (e[np.arange(H)[:, None], runs(r2, H)]), -0.75, 0.75))
    out_0 = unpack_weight(w3_words, w3_scales).T @ mxq(z, 0, "e4m3")
    return (out_0,) + planes(out_0)

@@ -1,0 +1,240 @@
+from contextlib import ExitStack
+
+import concourse.mybir as mybir
+from concourse.masks import make_identity
+
+K, T, S, N, H = 512, 2048, 512, 512, 512
+FLOPS = 2 * S * (2 * K * H + H * N)
+
+F32 = mybir.dt.float32
+BF16 = mybir.dt.bfloat16
+I32 = mybir.dt.int32
+U32 = mybir.dt.uint32
+U16 = mybir.dt.uint16
+U8 = mybir.dt.uint8
+FP8X4 = mybir.dt.float8_e4m3fn_x4
+ALU = mybir.AluOpType
+ACT = mybir.ActivationFunctionType
+
+P = 128
+PACK = 4
+BLOCK = 128
+CLIP = 0.75
+STRETCHES = ((0, 256), (256, 128), (384, 128))
+
+
+def tile_picked_bpclip_none_po_kernel(
+    tc, x_words, x_scales, w1_words, w1_scales, w2_words, w2_scales, gn, w3_words, w3_scales,
+    offs, p1, r1, p2, r2, out_0, out_1, out_2,
+):
+    nc = tc.nc
+
+    def words_of(dram):
+        return dram[0].rearrange("p n t -> p (n t)").bitcast(I32)
+
+    def load_scale_rows(queue, tile, dram, quadrant):
+        queue.dma_start(
+            out=tile[32 * quadrant : 32 * quadrant + 4, :].bitcast(I32),
+            in_=dram[0, 4 * quadrant : 4 * quadrant + 4, :].bitcast(I32),
+        )
+
+    with ExitStack() as ctx:
+        keep = ctx.enter_context(tc.tile_pool(name="keep", bufs=1))
+        ring = ctx.enter_context(tc.tile_pool(name="ring", bufs=2))
+        psum = ctx.enter_context(tc.psum_pool(name="psum", bufs=2))
+
+        lists = {}
+        for name in ("offs", "r1", "r2", "p1", "p2"):
+            lists[name] = keep.tile([P, S // 16], U16, name="list_" + name)
+        x_w = keep.tile([P, T], I32, align_bytes=64)
+        x_s = keep.tile([P, T], U8, align_bytes=64)
+        raw_w = [keep.tile([P, H], I32, name="raw_w%d" % i, align_bytes=64) for i in range(3)]
+        raw_s = [keep.tile([P, H], U8, name="raw_s%d" % i, align_bytes=64) for i in range(3)]
+        w_w = [keep.tile([P, H], I32, name="w_w%d" % i, align_bytes=64) for i in range(3)]
+        w_s = [keep.tile([P, H], U8, name="w_s%d" % i, align_bytes=64) for i in range(3)]
+        gain = keep.tile([P, PACK], F32)
+        upper = keep.tile([P, PACK], F32)
+        lower = keep.tile([P, PACK], F32)
+        ident = keep.tile([P, P], F32)
+
+        nc.vector.memset(x_s[:].bitcast(I32), 0)
+        nc.vector.memset(raw_s[1][:].bitcast(I32), 0)
+        nc.vector.memset(raw_s[0][:].bitcast(I32), 0)
+        nc.vector.memset(raw_s[2][:].bitcast(I32), 0)
+
+        nc.sync.dma_start(out=x_w[:], in_=words_of(x_words))
+        nc.sync.dma_start(lists["offs"][:], offs)
+        for q in range(4):
+            load_scale_rows(nc.scalar, x_s, x_scales, q)
+        nc.sync.dma_start(out=raw_w[1][:], in_=words_of(w2_words))
+        for q in range(4):
+            load_scale_rows(nc.scalar, raw_s[1], w2_scales, q)
+        nc.gpsimd.dma_start(out=gain[:], in_=gn.rearrange("(p t) o -> p (t o)", t=PACK))
+        nc.sync.dma_start(out=raw_w[0][:], in_=words_of(w1_words))
+        for q in range(4):
+            load_scale_rows(nc.scalar, raw_s[0], w1_scales, q)
+        nc.sync.dma_start(lists["r1"][:], r1)
+        nc.sync.dma_start(lists["r2"][:], r2)
+        nc.sync.dma_start(lists["p1"][:], p1)
+        nc.sync.dma_start(lists["p2"][:], p2)
+        nc.sync.dma_start(out=raw_w[2][:], in_=words_of(w3_words))
+        for q in range(4):
+            load_scale_rows(nc.gpsimd, raw_s[2], w3_scales, q)
+        make_identity(nc, ident[:])
+
+        def deal(i):
+            nc.vector.tensor_copy(
+                out=w_s[i][:].rearrange("p (t m) -> p t m", t=PACK),
+                in_=raw_s[i][:].rearrange("p (m t) -> p t m", t=PACK),
+            )
+            nc.vector.tensor_copy(
+                out=w_w[i][:].rearrange("p (t m) -> p t m", t=PACK),
+                in_=raw_w[i][:].rearrange("p (m t) -> p t m", t=PACK),
+            )
+
+        xq_w = keep.tile([P, S], U32, align_bytes=64)
+        xq_s = keep.tile([P, S], U8, align_bytes=64)
+        nc.vector.tensor_copy(xq_s[:], x_s[:].indirect(lists["offs"][:]))
+        nc.vector.tensor_copy(xq_w[:], x_w[:].bitcast(U32).indirect(lists["offs"][:]))
+        deal(1)
+        deal(0)
+        deal(2)
+
+        nc.scalar.activation(out=upper[:], in_=gain[:], func=ACT.Abs, scale=CLIP)
+        nc.scalar.activation(out=lower[:], in_=upper[:], func=ACT.Copy, scale=-1.0)
+
+        beliefs, messages = [], []
+        for t in range(PACK):
+            cols = slice(t * P, (t + 1) * P)
+            for i, name, into in ((1, "e", messages), (0, "y", beliefs)):
+                acc = psum.tile([P, S], F32, name="first")
+                nc.tensor.matmul_mx(
+                    out=acc[:],
+                    lhsT=w_w[i][:, cols].bitcast(FP8X4),
+                    lhsT_scale=w_s[i][:, cols],
+                    rhs=xq_w[:].bitcast(FP8X4),
+                    rhs_scale=xq_s[:],
+                    start=True,
+                    stop=True,
+                )
+                rows = keep.tile([P, S], F32, name="%s%d" % (name, t), align_bytes=64)
+                nc.scalar.activation(out=rows[:], in_=acc[:], func=ACT.Copy, scale=gain[:, t : t + 1])
+                into.append(rows)
+
+        out_words = keep.tile([P, S], I32, align_bytes=64)
+        out_scales = keep.tile([P, S], U8, align_bytes=64)
+        out_rows = out_0.rearrange("(p t) j -> p t j", t=PACK)
+
+        steps = [(j0, n, t) for j0, n in STRETCHES for t in range(PACK)]
+        shared = set()
+
+        def quantiser_input(step):
+            shared.add(step)
+            return keep.tile([P, BLOCK * PACK], BF16, name="before%d" % step, tag="step%d" % step, align_bytes=64)
+
+        def fetch_messages(step):
+            j0, n, t = steps[step]
+            if step in shared:
+                got = keep.tile([P, 2, n], F32, name="got%d" % step, tag="step%d" % step, align_bytes=64)
+            else:
+                got = ring.tile([P, 2, n], F32, name="got")
+            for c, name in enumerate(("r1", "r2")):
+                at = lists[name][:, j0 // 16 : (j0 + n) // 16]
+                nc.vector.tensor_copy(got[:, c, :], messages[t][:].indirect(at))
+            return got
+
+        def subtract(step, got):
+            j0, n, t = steps[step]
+            diff = ring.tile([P, 2, n], F32, name="diff")
+            for c, name in enumerate(("p1", "p2")):
+                at = lists[name][:, j0 // 16 : (j0 + n) // 16]
+                nc.vector.tensor_tensor(diff[:, c, :], beliefs[t][:].indirect(at), got[:, c, :], ALU.subtract)
+            return diff
+
+        due = {}
+        banks = {}
+
+        def clip_and_sum(step, diff):
+            j0, n, t = steps[step]
+            clipped = ring.tile([P, 2, n], F32, name="clipped")
+            nc.vector.tensor_scalar(
+                clipped[:], diff[:], lower[:, t : t + 1], upper[:, t : t + 1], ALU.max, ALU.min
+            )
+            for b in range(n // BLOCK):
+                lo = b * BLOCK
+                if t == 0:
+                    banks[b] = (psum.tile([P, PACK, P], F32, name="sums"), psum.tile([P, 2, BLOCK], F32, name="turned"))
+                sums, turned = banks[b]
+                terms = (
+                    beliefs[t][:, j0 + lo : j0 + lo + BLOCK],
+                    clipped[:, 0, lo : lo + BLOCK],
+                    clipped[:, 1, lo : lo + BLOCK],
+                )
+                for c, term in enumerate(terms):
+                    nc.tensor.matmul(
+                        sums[:, t, :], lhsT=term, rhs=ident[:], is_transpose=True,
+                        start=(c == 0), stop=(c == len(terms) - 1),
+                    )
+            if t % 2 == 0:
+                return
+            for b in range(n // BLOCK):
+                sums, turned = banks[b]
+                pairs = ring.tile([P, P, 2], BF16, name="pairs", align_bytes=64)
+                nc.scalar.copy(out=pairs[:], in_=sums[:, t - 1 : t + 1, :].rearrange("j e p -> j p e"))
+                nc.tensor.transpose(turned[:, t // 2, :], pairs[:].rearrange("j p e -> j (p e)").bitcast(F32), ident[:])
+                if t == PACK - 1:
+                    at = step + 3 + b
+                    z_in = quantiser_input(at)
+                    nc.scalar.copy(
+                        out=z_in[:].bitcast(F32).rearrange("p (j u) -> p j u", u=2),
+                        in_=turned[:].rearrange("p u j -> p j u"),
+                    )
+                    due.setdefault(at, []).append(lambda j=j0 + b * BLOCK, z_in=z_in, at=at: second_product(j, z_in, at))
+
+        def second_product(j0, z_in, step):
+            cols = slice(j0, j0 + BLOCK)
+            z_w = ring.tile([P, BLOCK], U32, name="z_w", align_bytes=64)
+            z_s = ring.tile([P, BLOCK], U8, name="z_s", align_bytes=64)
+            nc.vector.quantize_mx(out=z_w[:].bitcast(FP8X4), scales=z_s[:], in_=z_in[:])
+            acc = psum.tile([P, PACK, BLOCK], F32, name="second")
+            for t in range(PACK):
+                nc.tensor.matmul_mx(
+                    out=acc[:, t, :],
+                    lhsT=w_w[2][:, t * P : (t + 1) * P].bitcast(FP8X4),
+                    lhsT_scale=w_s[2][:, t * P : (t + 1) * P],
+                    rhs=z_w[:].bitcast(FP8X4),
+                    rhs_scale=z_s[:],
+                    start=True,
+                    stop=True,
+                )
+            result = ring.tile([P, PACK, BLOCK], F32, name="result")
+            nc.scalar.copy(out=result[:], in_=acc[:])
+            nc.sync.dma_start(out=out_rows[:, :, cols], in_=result[:])
+            rounded = quantiser_input(step + 2)
+            if j0 + BLOCK < S:
+                nc.scalar.copy(out=rounded[:].rearrange("p (j t) -> p j t", t=PACK), in_=acc[:].rearrange("p t j -> p j t"))
+            else:
+                nc.vector.tensor_copy(
+                    out=rounded[:].rearrange("p (c i t) -> p c t i", t=PACK, i=4),
+                    in_=result[:].rearrange("p t (c i) -> p c t i", i=4),
+                )
+            due.setdefault(step + 2, []).append(lambda: hand_on(cols, rounded))
+
+        def hand_on(cols, rounded):
+            nc.vector.quantize_mx(out=out_words[:, cols].bitcast(FP8X4), scales=out_scales[:, cols], in_=rounded[:])
+            nc.sync.dma_start(out=words_of(out_1)[:, cols], in_=out_words[:, cols])
+
+        diff = None
+        for step in range(len(steps) + 5):
+            for work in due.get(step, []):
+                work()
+            got = fetch_messages(step) if step < len(steps) else None
+            if diff is not None:
+                clip_and_sum(step - 1, diff)
+            diff = subtract(step, got) if step < len(steps) else None
+
+        for q in range(4):
+            (nc.sync if q % 2 == 0 else nc.scalar).dma_start(
+                out=out_2[0, 4 * q : 4 * q + 4, :].bitcast(I32),
+                in_=out_scales[32 * q : 32 * q + 4, :].bitcast(I32),
+            )

@@ -20,6 +20,7 @@ P = 128
 PACK = 4
 BLOCK = 128
 CLIP = 0.75
+HALF = S // 2
 STRETCHES = ((0, 256), (256, 128), (384, 128))
 
 
@@ -34,8 +35,8 @@ def tile_picked_bpclip_none_po_kernel(
 
     def load_scale_rows(queue, tile, dram, quadrant):
         queue.dma_start(
-            out=tile[32 * quadrant : 32 * quadrant + 4, :].bitcast(I32),
-            in_=dram[0, 4 * quadrant : 4 * quadrant + 4, :].bitcast(I32),
+            out=tile[32 * quadrant : 32 * quadrant + 32, :].bitcast(I32),
+            in_=dram[0, 4 * quadrant : 4 * quadrant + 4, :].bitcast(I32).partition_broadcast(8),
         )
 
     with ExitStack() as ctx:
@@ -46,59 +47,57 @@ def tile_picked_bpclip_none_po_kernel(
         lists = {}
         for name in ("offs", "r1", "r2", "p1", "p2"):
             lists[name] = keep.tile([P, S // 16], U16, name="list_" + name)
-        x_w = keep.tile([P, T], I32, align_bytes=64)
+        x_w = keep.tile([P, T], I32, tag="dealt_s0", align_bytes=64)
         x_s = keep.tile([P, T], U8, align_bytes=64)
         raw_w = [keep.tile([P, H], I32, name="raw_w%d" % i, align_bytes=64) for i in range(3)]
         raw_s = [keep.tile([P, H], U8, name="raw_s%d" % i, align_bytes=64) for i in range(3)]
-        w_w = [keep.tile([P, H], I32, name="w_w%d" % i, align_bytes=64) for i in range(3)]
-        w_s = [keep.tile([P, H], U8, name="w_s%d" % i, align_bytes=64) for i in range(3)]
+        w_w = [keep.tile([P, H], I32, name="w_w%d" % i, align_bytes=64) for i in range(2)]
+        w_s = [keep.tile([P, H], U8, name="w_s%d" % i, tag="dealt_s%d" % i, align_bytes=64) for i in range(2)]
         gain = keep.tile([P, PACK], F32)
         upper = keep.tile([P, PACK], F32)
         lower = keep.tile([P, PACK], F32)
         ident = keep.tile([P, P], F32)
 
-        nc.vector.memset(x_s[:].bitcast(I32), 0)
-        nc.vector.memset(raw_s[1][:].bitcast(I32), 0)
-        nc.vector.memset(raw_s[0][:].bitcast(I32), 0)
-        nc.vector.memset(raw_s[2][:].bitcast(I32), 0)
-
-        nc.sync.dma_start(out=x_w[:], in_=words_of(x_words))
-        nc.sync.dma_start(lists["offs"][:], offs)
         for q in range(4):
-            load_scale_rows(nc.scalar, x_s, x_scales, q)
+            load_scale_rows(nc.sync, x_s, x_scales, q)
+        nc.sync.dma_start(lists["offs"][:], offs)
+        nc.sync.dma_start(out=x_w[:], in_=words_of(x_words))
         nc.sync.dma_start(out=raw_w[1][:], in_=words_of(w2_words))
         for q in range(4):
-            load_scale_rows(nc.scalar, raw_s[1], w2_scales, q)
-        nc.gpsimd.dma_start(out=gain[:], in_=gn.rearrange("(p t) o -> p (t o)", t=PACK))
+            load_scale_rows(nc.sync, raw_s[1], w2_scales, q)
+        nc.scalar.dma_start(out=gain[:], in_=gn.rearrange("(p t) o -> p (t o)", t=PACK))
         nc.sync.dma_start(out=raw_w[0][:], in_=words_of(w1_words))
         for q in range(4):
-            load_scale_rows(nc.scalar, raw_s[0], w1_scales, q)
+            load_scale_rows(nc.gpsimd, raw_s[0], w1_scales, q)
         nc.sync.dma_start(lists["r1"][:], r1)
         nc.sync.dma_start(lists["r2"][:], r2)
         nc.sync.dma_start(lists["p1"][:], p1)
         nc.sync.dma_start(lists["p2"][:], p2)
         nc.sync.dma_start(out=raw_w[2][:], in_=words_of(w3_words))
         for q in range(4):
-            load_scale_rows(nc.gpsimd, raw_s[2], w3_scales, q)
+            load_scale_rows(nc.sync, raw_s[2], w3_scales, q)
         make_identity(nc, ident[:])
 
-        def deal(i):
+        def deal(i, ts=slice(0, PACK)):
             nc.vector.tensor_copy(
-                out=w_s[i][:].rearrange("p (t m) -> p t m", t=PACK),
-                in_=raw_s[i][:].rearrange("p (m t) -> p t m", t=PACK),
+                out=w_w[i][:].rearrange("p (t c i) -> p c t i", t=PACK, i=4)[:, :, ts, :],
+                in_=raw_w[i][:].rearrange("p (c i t) -> p c t i", t=PACK, i=4)[:, :, ts, :],
             )
             nc.vector.tensor_copy(
-                out=w_w[i][:].rearrange("p (t m) -> p t m", t=PACK),
-                in_=raw_w[i][:].rearrange("p (m t) -> p t m", t=PACK),
+                out=w_s[i][:].rearrange("p (t m) -> p t m", t=PACK)[:, ts, :],
+                in_=raw_s[i][:].rearrange("p (m t) -> p t m", t=PACK)[:, ts, :],
             )
 
         xq_w = keep.tile([P, S], U32, align_bytes=64)
         xq_s = keep.tile([P, S], U8, align_bytes=64)
         nc.vector.tensor_copy(xq_s[:], x_s[:].indirect(lists["offs"][:]))
-        nc.vector.tensor_copy(xq_w[:], x_w[:].bitcast(U32).indirect(lists["offs"][:]))
-        deal(1)
+        for h in range(2):
+            nc.vector.tensor_copy(
+                xq_w[:, h * HALF : (h + 1) * HALF],
+                x_w[:].bitcast(U32).indirect(lists["offs"][:, h * HALF // 16 : (h + 1) * HALF // 16]),
+            )
+            deal(1, slice(0, 2) if h == 0 else slice(2, PACK))
         deal(0)
-        deal(2)
 
         nc.scalar.activation(out=upper[:], in_=gain[:], func=ACT.Abs, scale=CLIP)
         nc.scalar.activation(out=lower[:], in_=upper[:], func=ACT.Copy, scale=-1.0)
@@ -107,18 +106,22 @@ def tile_picked_bpclip_none_po_kernel(
         for t in range(PACK):
             cols = slice(t * P, (t + 1) * P)
             for i, name, into in ((1, "e", messages), (0, "y", beliefs)):
-                acc = psum.tile([P, S], F32, name="first")
-                nc.tensor.matmul_mx(
-                    out=acc[:],
-                    lhsT=w_w[i][:, cols].bitcast(FP8X4),
-                    lhsT_scale=w_s[i][:, cols],
-                    rhs=xq_w[:].bitcast(FP8X4),
-                    rhs_scale=xq_s[:],
-                    start=True,
-                    stop=True,
-                )
                 rows = keep.tile([P, S], F32, name="%s%d" % (name, t), align_bytes=64)
-                nc.scalar.activation(out=rows[:], in_=acc[:], func=ACT.Copy, scale=gain[:, t : t + 1])
+                width = HALF if not messages else S
+                for j0 in range(0, S, width):
+                    acc = psum.tile([P, width], F32, name="first")
+                    nc.tensor.matmul_mx(
+                        out=acc[:],
+                        lhsT=w_w[i][:, cols].bitcast(FP8X4),
+                        lhsT_scale=w_s[i][:, cols],
+                        rhs=xq_w[:, j0 : j0 + width].bitcast(FP8X4),
+                        rhs_scale=xq_s[:, j0 : j0 + width],
+                        start=True,
+                        stop=True,
+                    )
+                    nc.scalar.activation(
+                        out=rows[:, j0 : j0 + width], in_=acc[:], func=ACT.Copy, scale=gain[:, t : t + 1]
+                    )
                 into.append(rows)
 
         out_words = keep.tile([P, S], I32, align_bytes=64)
@@ -126,18 +129,22 @@ def tile_picked_bpclip_none_po_kernel(
         out_rows = out_0.rearrange("(p t) j -> p t j", t=PACK)
 
         steps = [(j0, n, t) for j0, n in STRETCHES for t in range(PACK)]
-        shared = set()
+        shared = {"got1", "diff1"}
 
-        def quantiser_input(step):
-            shared.add(step)
-            return keep.tile([P, BLOCK * PACK], BF16, name="before%d" % step, tag="step%d" % step, align_bytes=64)
+        def quantiser_input(tag):
+            shared.add(tag)
+            return keep.tile([P, BLOCK * PACK], BF16, name="before_" + tag, tag=tag, align_bytes=64)
+
+        def gathered(kind, step):
+            tag = "%s%d" % (kind, step)
+            shape = [P, 2, steps[step][1]]
+            if tag in shared:
+                return keep.tile(shape, F32, name=tag, tag=tag, align_bytes=64)
+            return ring.tile(shape, F32, name=kind)
 
         def fetch_messages(step):
             j0, n, t = steps[step]
-            if step in shared:
-                got = keep.tile([P, 2, n], F32, name="got%d" % step, tag="step%d" % step, align_bytes=64)
-            else:
-                got = ring.tile([P, 2, n], F32, name="got")
+            got = gathered("got", step)
             for c, name in enumerate(("r1", "r2")):
                 at = lists[name][:, j0 // 16 : (j0 + n) // 16]
                 nc.vector.tensor_copy(got[:, c, :], messages[t][:].indirect(at))
@@ -145,21 +152,48 @@ def tile_picked_bpclip_none_po_kernel(
 
         def subtract(step, got):
             j0, n, t = steps[step]
-            diff = ring.tile([P, 2, n], F32, name="diff")
+            diff = gathered("diff", step)
             for c, name in enumerate(("p1", "p2")):
                 at = lists[name][:, j0 // 16 : (j0 + n) // 16]
                 nc.vector.tensor_tensor(diff[:, c, :], beliefs[t][:].indirect(at), got[:, c, :], ALU.subtract)
             return diff
 
-        due = {}
+        before_fetch, before_subtract = {}, {}
         banks = {}
+        last_clipped = keep.tile([P, 2, 2, BLOCK], F32)
+        last_partial = keep.tile([P, 2, BLOCK], F32)
+        last_z = keep.tile([P, BLOCK * PACK], BF16, align_bytes=64)
+
+        def clip(out, diff, t):
+            nc.vector.tensor_scalar(out, diff, lower[:, t : t + 1], upper[:, t : t + 1], ALU.max, ALU.min)
+
+        def sum_on_vector(step, diff):
+            j0, n, t = steps[step]
+            e = t - 2
+            if t == 2:
+                clip(last_clipped[:, :, e, :], diff[:], t)
+            else:
+                for c in range(2):
+                    clip(last_clipped[:, c, e, :], diff[:, c, :], t)
+            nc.vector.tensor_tensor(
+                last_partial[:, e, :], beliefs[t][:, j0 : j0 + n], last_clipped[:, 0, e, :], ALU.add
+            )
+            if t == PACK - 1:
+                nc.vector.tensor_tensor(
+                    last_z[:].rearrange("p (c i t) -> p c t i", t=PACK, i=4)[:, :, 2:4, :],
+                    last_partial[:].rearrange("p e (c i) -> p c e i", i=4),
+                    last_clipped[:, 1, :, :].rearrange("p e (c i) -> p c e i", i=4),
+                    ALU.add,
+                )
+                second_product(j0, last_z, step)
 
         def clip_and_sum(step, diff):
             j0, n, t = steps[step]
-            clipped = ring.tile([P, 2, n], F32, name="clipped")
-            nc.vector.tensor_scalar(
-                clipped[:], diff[:], lower[:, t : t + 1], upper[:, t : t + 1], ALU.max, ALU.min
-            )
+            last = j0 + n == S
+            if last and t >= 2:
+                return sum_on_vector(step, diff)
+            clipped = ring.tile([P, 2, n], F32, name="clipped", bufs=3)
+            clip(clipped[:], diff[:], t)
             for b in range(n // BLOCK):
                 lo = b * BLOCK
                 if t == 0:
@@ -182,24 +216,29 @@ def tile_picked_bpclip_none_po_kernel(
                 pairs = ring.tile([P, P, 2], BF16, name="pairs", align_bytes=64)
                 nc.scalar.copy(out=pairs[:], in_=sums[:, t - 1 : t + 1, :].rearrange("j e p -> j p e"))
                 nc.tensor.transpose(turned[:, t // 2, :], pairs[:].rearrange("j p e -> j (p e)").bitcast(F32), ident[:])
-                if t == PACK - 1:
-                    at = step + 3 + b
-                    z_in = quantiser_input(at)
+                if last:
+                    nc.scalar.copy(
+                        out=last_z[:].bitcast(F32).rearrange("p (j u) -> p j u", u=2)[:, :, 0], in_=turned[:, 0, :]
+                    )
+                elif t == PACK - 1:
+                    at = step + 4 + b
+                    z_in = quantiser_input("got%d" % at)
                     nc.scalar.copy(
                         out=z_in[:].bitcast(F32).rearrange("p (j u) -> p j u", u=2),
                         in_=turned[:].rearrange("p u j -> p j u"),
                     )
-                    due.setdefault(at, []).append(lambda j=j0 + b * BLOCK, z_in=z_in, at=at: second_product(j, z_in, at))
+                    before_fetch[at] = lambda j=j0 + b * BLOCK, z_in=z_in, at=at: second_product(j, z_in, at)
 
         def second_product(j0, z_in, step):
             cols = slice(j0, j0 + BLOCK)
             z_w = ring.tile([P, BLOCK], U32, name="z_w", align_bytes=64)
             z_s = ring.tile([P, BLOCK], U8, name="z_s", align_bytes=64)
             nc.vector.quantize_mx(out=z_w[:].bitcast(FP8X4), scales=z_s[:], in_=z_in[:])
-            acc = psum.tile([P, PACK, BLOCK], F32, name="second")
+            last = j0 + BLOCK == S
+            accs = [psum.tile([P, PACK, BLOCK], F32, name="second") for half in range(2 if last else 1)]
             for t in range(PACK):
                 nc.tensor.matmul_mx(
-                    out=acc[:, t, :],
+                    out=accs[t // 2 if last else 0][:, t, :],
                     lhsT=w_w[2][:, t * P : (t + 1) * P].bitcast(FP8X4),
                     lhsT_scale=w_s[2][:, t * P : (t + 1) * P],
                     rhs=z_w[:].bitcast(FP8X4),
@@ -208,30 +247,47 @@ def tile_picked_bpclip_none_po_kernel(
                     stop=True,
                 )
             result = ring.tile([P, PACK, BLOCK], F32, name="result")
-            nc.scalar.copy(out=result[:], in_=acc[:])
-            nc.sync.dma_start(out=out_rows[:, :, cols], in_=result[:])
-            rounded = quantiser_input(step + 2)
-            if j0 + BLOCK < S:
-                nc.scalar.copy(out=rounded[:].rearrange("p (j t) -> p j t", t=PACK), in_=acc[:].rearrange("p t j -> p j t"))
+            rounded = quantiser_input("diff%d" % (step + 2 + last))
+            if not last:
+                nc.scalar.copy(out=result[:], in_=accs[0][:])
+                nc.sync.dma_start(out=out_rows[:, :, cols], in_=result[:])
+                nc.scalar.copy(
+                    out=rounded[:].rearrange("p (j t) -> p j t", t=PACK), in_=accs[0][:].rearrange("p t j -> p j t")
+                )
+                before_subtract[step + 2] = lambda: hand_on(cols, rounded)
             else:
+                nc.scalar.copy(out=result[:, 0:2, :], in_=accs[0][:, 0:2, :])
+                nc.scalar.dma_start(out=out_rows[:, 0:2, cols], in_=result[:, 0:2, :])
+                nc.vector.tensor_copy(out=result[:, 2:4, :], in_=accs[1][:, 2:4, :])
+                nc.sync.dma_start(out=out_rows[:, 2:4, cols], in_=result[:, 2:4, :])
+                before_subtract[len(steps) + 1]()
                 nc.vector.tensor_copy(
                     out=rounded[:].rearrange("p (c i t) -> p c t i", t=PACK, i=4),
                     in_=result[:].rearrange("p t (c i) -> p c t i", i=4),
                 )
-            due.setdefault(step + 2, []).append(lambda: hand_on(cols, rounded))
+                hand_on(cols, rounded)
 
         def hand_on(cols, rounded):
             nc.vector.quantize_mx(out=out_words[:, cols].bitcast(FP8X4), scales=out_scales[:, cols], in_=rounded[:])
             nc.sync.dma_start(out=words_of(out_1)[:, cols], in_=out_words[:, cols])
 
+        def deal_w3():
+            w_w.append(keep.tile([P, H], I32, name="w_w2", tag="got1", align_bytes=64))
+            w_s.append(keep.tile([P, H], U8, name="w_s2", tag="diff1", align_bytes=64))
+            deal(2)
+
+        before_subtract[2] = deal_w3
         diff = None
-        for step in range(len(steps) + 5):
-            for work in due.get(step, []):
-                work()
-            got = fetch_messages(step) if step < len(steps) else None
+        for step in range(len(steps)):
+            if step in before_fetch:
+                before_fetch[step]()
+            got = fetch_messages(step)
             if diff is not None:
                 clip_and_sum(step - 1, diff)
-            diff = subtract(step, got) if step < len(steps) else None
+            if step in before_subtract:
+                before_subtract[step]()
+            diff = subtract(step, got)
+        clip_and_sum(len(steps) - 1, diff)
 
         for q in range(4):
             (nc.sync if q % 2 == 0 else nc.scalar).dma_start(

@@ -42,6 +42,7 @@ def tile_picked_bpclip_none_po_kernel(
     with ExitStack() as ctx:
         keep = ctx.enter_context(tc.tile_pool(name="keep", bufs=1))
         ring = ctx.enter_context(tc.tile_pool(name="ring", bufs=2))
+        deep = ctx.enter_context(tc.tile_pool(name="deep", bufs=4))
         psum = ctx.enter_context(tc.psum_pool(name="psum", bufs=2))
 
         lists = {}
@@ -68,7 +69,7 @@ def tile_picked_bpclip_none_po_kernel(
         nc.scalar.dma_start(out=gain[:], in_=gn.rearrange("(p t) o -> p (t o)", t=PACK))
         nc.sync.dma_start(out=raw_w[0][:], in_=words_of(w1_words))
         for q in range(4):
-            load_scale_rows(nc.gpsimd, raw_s[0], w1_scales, q)
+            load_scale_rows((nc.scalar, nc.sync, nc.gpsimd, nc.gpsimd)[q], raw_s[0], w1_scales, q)
         nc.sync.dma_start(lists["r1"][:], r1)
         nc.sync.dma_start(lists["r2"][:], r2)
         nc.sync.dma_start(lists["p1"][:], p1)
@@ -106,7 +107,9 @@ def tile_picked_bpclip_none_po_kernel(
         for t in range(PACK):
             cols = slice(t * P, (t + 1) * P)
             for i, name, into in ((1, "e", messages), (0, "y", beliefs)):
-                rows = keep.tile([P, S], F32, name="%s%d" % (name, t), align_bytes=64)
+                rows = keep.tile([P, 2 * S if i == 1 else S], F32, name="%s%d" % (name, t), align_bytes=64)
+                if i == 1:
+                    nc.vector.memset(rows[:, S:], 0.0)
                 width = HALF if not messages else S
                 for j0 in range(0, S, width):
                     acc = psum.tile([P, width], F32, name="first")
@@ -129,33 +132,32 @@ def tile_picked_bpclip_none_po_kernel(
         out_rows = out_0.rearrange("(p t) j -> p t j", t=PACK)
 
         steps = [(j0, n, t) for j0, n in STRETCHES for t in range(PACK)]
-        shared = {"got1", "diff1"}
+        shared = {"diff0", "diff1"}
 
         def quantiser_input(tag):
             shared.add(tag)
             return keep.tile([P, BLOCK * PACK], BF16, name="before_" + tag, tag=tag, align_bytes=64)
 
-        def gathered(kind, step):
-            tag = "%s%d" % (kind, step)
-            shape = [P, 2, steps[step][1]]
-            if tag in shared:
-                return keep.tile(shape, F32, name=tag, tag=tag, align_bytes=64)
-            return ring.tile(shape, F32, name=kind)
+        fetched = []
 
-        def fetch_messages(step):
-            j0, n, t = steps[step]
-            got = gathered("got", step)
+        def fetch_messages(t):
+            got = keep.tile([P, 2, S], F32, name="got%d" % t)
             for c, name in enumerate(("r1", "r2")):
-                at = lists[name][:, j0 // 16 : (j0 + n) // 16]
-                nc.vector.tensor_copy(got[:, c, :], messages[t][:].indirect(at))
-            return got
+                nc.vector.tensor_copy(got[:, c, :], messages[t][:].indirect(lists[name][:]))
+            fetched.append(got)
 
-        def subtract(step, got):
+        def subtract(step):
             j0, n, t = steps[step]
-            diff = gathered("diff", step)
+            tag = "diff%d" % step
+            if tag in shared:
+                diff = keep.tile([P, 2, n], F32, name=tag, tag=tag, align_bytes=64)
+            else:
+                diff = ring.tile([P, 2, n], F32, name="diff", bufs=3)
             for c, name in enumerate(("p1", "p2")):
                 at = lists[name][:, j0 // 16 : (j0 + n) // 16]
-                nc.vector.tensor_tensor(diff[:, c, :], beliefs[t][:].indirect(at), got[:, c, :], ALU.subtract)
+                nc.vector.tensor_tensor(
+                    diff[:, c, :], beliefs[t][:].indirect(at), fetched[t][:, c, j0 : j0 + n], ALU.subtract
+                )
             return diff
 
         before_fetch, before_subtract = {}, {}
@@ -192,7 +194,7 @@ def tile_picked_bpclip_none_po_kernel(
             last = j0 + n == S
             if last and t >= 2:
                 return sum_on_vector(step, diff)
-            clipped = ring.tile([P, 2, n], F32, name="clipped", bufs=3)
+            clipped = keep.tile([P, 2, n], F32, name="clipped%d" % step)
             clip(clipped[:], diff[:], t)
             for b in range(n // BLOCK):
                 lo = b * BLOCK
@@ -213,7 +215,7 @@ def tile_picked_bpclip_none_po_kernel(
                 return
             for b in range(n // BLOCK):
                 sums, turned = banks[b]
-                pairs = ring.tile([P, P, 2], BF16, name="pairs", align_bytes=64)
+                pairs = deep.tile([P, P, 2], BF16, name="pairs", align_bytes=64)
                 nc.scalar.copy(out=pairs[:], in_=sums[:, t - 1 : t + 1, :].rearrange("j e p -> j p e"))
                 nc.tensor.transpose(turned[:, t // 2, :], pairs[:].rearrange("j p e -> j (p e)").bitcast(F32), ident[:])
                 if last:
@@ -221,8 +223,8 @@ def tile_picked_bpclip_none_po_kernel(
                         out=last_z[:].bitcast(F32).rearrange("p (j u) -> p j u", u=2)[:, :, 0], in_=turned[:, 0, :]
                     )
                 elif t == PACK - 1:
-                    at = step + 4 + b
-                    z_in = quantiser_input("got%d" % at)
+                    at = step + 5 + b
+                    z_in = quantiser_input("diff%d" % at)
                     nc.scalar.copy(
                         out=z_in[:].bitcast(F32).rearrange("p (j u) -> p j u", u=2),
                         in_=turned[:].rearrange("p u j -> p j u"),
@@ -231,8 +233,8 @@ def tile_picked_bpclip_none_po_kernel(
 
         def second_product(j0, z_in, step):
             cols = slice(j0, j0 + BLOCK)
-            z_w = ring.tile([P, BLOCK], U32, name="z_w", align_bytes=64)
-            z_s = ring.tile([P, BLOCK], U8, name="z_s", align_bytes=64)
+            z_w = deep.tile([P, BLOCK], U32, name="z_w", align_bytes=64)
+            z_s = deep.tile([P, BLOCK], U8, name="z_s", align_bytes=64)
             nc.vector.quantize_mx(out=z_w[:].bitcast(FP8X4), scales=z_s[:], in_=z_in[:])
             last = j0 + BLOCK == S
             accs = [psum.tile([P, PACK, BLOCK], F32, name="second") for half in range(2 if last else 1)]
@@ -246,8 +248,8 @@ def tile_picked_bpclip_none_po_kernel(
                     start=True,
                     stop=True,
                 )
-            result = ring.tile([P, PACK, BLOCK], F32, name="result")
-            rounded = quantiser_input("diff%d" % (step + 2 + last))
+            result = deep.tile([P, PACK, BLOCK], F32, name="result")
+            rounded = deep.tile([P, BLOCK * PACK], BF16, name="rounded", align_bytes=64)
             if not last:
                 nc.scalar.copy(out=result[:], in_=accs[0][:])
                 nc.sync.dma_start(out=out_rows[:, :, cols], in_=result[:])
@@ -260,7 +262,7 @@ def tile_picked_bpclip_none_po_kernel(
                 nc.scalar.dma_start(out=out_rows[:, 0:2, cols], in_=result[:, 0:2, :])
                 nc.vector.tensor_copy(out=result[:, 2:4, :], in_=accs[1][:, 2:4, :])
                 nc.sync.dma_start(out=out_rows[:, 2:4, cols], in_=result[:, 2:4, :])
-                before_subtract[len(steps) + 1]()
+                before_subtract[len(steps) + 2]()
                 nc.vector.tensor_copy(
                     out=rounded[:].rearrange("p (c i t) -> p c t i", t=PACK, i=4),
                     in_=result[:].rearrange("p t (c i) -> p c t i", i=4),
@@ -272,22 +274,25 @@ def tile_picked_bpclip_none_po_kernel(
             nc.sync.dma_start(out=words_of(out_1)[:, cols], in_=out_words[:, cols])
 
         def deal_w3():
-            w_w.append(keep.tile([P, H], I32, name="w_w2", tag="got1", align_bytes=64))
+            w_w.append(keep.tile([P, H], I32, name="w_w2", tag="diff0", align_bytes=64))
             w_s.append(keep.tile([P, H], U8, name="w_s2", tag="diff1", align_bytes=64))
             deal(2)
 
-        before_subtract[2] = deal_w3
-        diff = None
+        before_subtract[3] = deal_w3
+        waiting = None
         for step in range(len(steps)):
+            if step < PACK:
+                fetch_messages(step)
             if step in before_fetch:
                 before_fetch[step]()
-            got = fetch_messages(step)
-            if diff is not None:
-                clip_and_sum(step - 1, diff)
             if step in before_subtract:
                 before_subtract[step]()
-            diff = subtract(step, got)
-        clip_and_sum(len(steps) - 1, diff)
+            diff = subtract(step)
+            if waiting is not None:
+                clip_and_sum(step - 1, waiting)
+            waiting = diff
+        before_fetch[len(steps)]()
+        clip_and_sum(len(steps) - 1, waiting)
 
         for q in range(4):
             (nc.sync if q % 2 == 0 else nc.scalar).dma_start(

@@ -169,31 +169,41 @@ def tile_picked_bpclip_none_po_kernel(
         def clip(out, diff, t):
             nc.vector.tensor_scalar(out, diff, lower[:, t : t + 1], upper[:, t : t + 1], ALU.max, ALU.min)
 
-        def sum_on_vector(step, diff):
-            j0, n, t = steps[step]
-            e = t - 2
-            if t == 2:
-                clip(last_clipped[:, :, e, :], diff[:], t)
-            else:
-                for c in range(2):
-                    clip(last_clipped[:, c, e, :], diff[:, c, :], t)
-            nc.vector.tensor_tensor(
-                last_partial[:, e, :], beliefs[t][:, j0 : j0 + n], last_clipped[:, 0, e, :], ALU.add
-            )
-            if t == PACK - 1:
+        def last_pair(waiting):
+            j0, n = STRETCHES[-1]
+            diff = ring.tile([P, 2, 2, n], F32, name="diff", bufs=3)
+
+            def difference(c, e):
+                at = lists[("p1", "p2")[c]][:, j0 // 16 : (j0 + n) // 16]
                 nc.vector.tensor_tensor(
-                    last_z[:].rearrange("p (c i t) -> p c t i", t=PACK, i=4)[:, :, 2:4, :],
-                    last_partial[:].rearrange("p e (c i) -> p c e i", i=4),
-                    last_clipped[:, 1, :, :].rearrange("p e (c i) -> p c e i", i=4),
-                    ALU.add,
+                    diff[:, c, e, :], beliefs[2 + e][:].indirect(at), fetched[2 + e][:, c, j0 : j0 + n], ALU.subtract
                 )
-                second_product(j0, last_z, step)
+
+            difference(0, 0)
+            difference(0, 1)
+            clip_and_sum(len(steps) - 3, waiting)
+            difference(1, 0)
+            for e in range(2):
+                clip(last_clipped[:, 0, e, :], diff[:, 0, e, :], 2 + e)
+            for e in range(2):
+                nc.vector.tensor_tensor(
+                    last_partial[:, e, :], beliefs[2 + e][:, j0 : j0 + n], last_clipped[:, 0, e, :], ALU.add
+                )
+            difference(1, 1)
+            for e in range(2):
+                clip(last_clipped[:, 1, e, :], diff[:, 1, e, :], 2 + e)
+            before_fetch[len(steps)]()
+            nc.vector.tensor_tensor(
+                last_z[:].rearrange("p (c i t) -> p c t i", t=PACK, i=4)[:, :, 2:4, :],
+                last_partial[:].rearrange("p e (c i) -> p c e i", i=4),
+                last_clipped[:, 1, :, :].rearrange("p e (c i) -> p c e i", i=4),
+                ALU.add,
+            )
+            second_product(j0, last_z, len(steps))
 
         def clip_and_sum(step, diff):
             j0, n, t = steps[step]
             last = j0 + n == S
-            if last and t >= 2:
-                return sum_on_vector(step, diff)
             clipped = keep.tile([P, 2, n], F32, name="clipped%d" % step)
             clip(clipped[:], diff[:], t)
             for b in range(n // BLOCK):
@@ -223,7 +233,7 @@ def tile_picked_bpclip_none_po_kernel(
                         out=last_z[:].bitcast(F32).rearrange("p (j u) -> p j u", u=2)[:, :, 0], in_=turned[:, 0, :]
                     )
                 elif t == PACK - 1:
-                    at = step + 5 + b
+                    at = step + 4 + b + (step > PACK)
                     z_in = quantiser_input("diff%d" % at)
                     nc.scalar.copy(
                         out=z_in[:].bitcast(F32).rearrange("p (j u) -> p j u", u=2),
@@ -237,7 +247,7 @@ def tile_picked_bpclip_none_po_kernel(
             z_s = deep.tile([P, BLOCK], U8, name="z_s", align_bytes=64)
             nc.vector.quantize_mx(out=z_w[:].bitcast(FP8X4), scales=z_s[:], in_=z_in[:])
             last = j0 + BLOCK == S
-            accs = [psum.tile([P, PACK, BLOCK], F32, name="second") for half in range(2 if last else 1)]
+            accs = [psum.tile([P, PACK, BLOCK], F32, name="first" if last else "second") for half in range(2 if last else 1)]
             for t in range(PACK):
                 nc.tensor.matmul_mx(
                     out=accs[t // 2 if last else 0][:, t, :],
@@ -280,7 +290,7 @@ def tile_picked_bpclip_none_po_kernel(
 
         before_subtract[3] = deal_w3
         waiting = None
-        for step in range(len(steps)):
+        for step in range(len(steps) - 2):
             if step < PACK:
                 fetch_messages(step)
             if step in before_fetch:
@@ -291,8 +301,8 @@ def tile_picked_bpclip_none_po_kernel(
             if waiting is not None:
                 clip_and_sum(step - 1, waiting)
             waiting = diff
-        before_fetch[len(steps)]()
-        clip_and_sum(len(steps) - 1, waiting)
+        before_subtract[len(steps) - 2]()
+        last_pair(waiting)
 
         for q in range(4):
             (nc.sync if q % 2 == 0 else nc.scalar).dma_start(

@@ -18,10 +18,16 @@ ACT = mybir.ActivationFunctionType
 
 P = 128
 PACK = 4
-BLOCK = 128
+QUADRANTS = 4
+GROUP = 16
+LINE = 4
 CLIP = 0.75
 HALF = S // 2
-STRETCHES = ((0, 256), (256, 128), (384, 128))
+BLOCK = 128
+STRETCHES = ((0, 2 * BLOCK), (2 * BLOCK, BLOCK), (3 * BLOCK, BLOCK))
+MULTIPLY_LAG = 4
+HAND_ON_LAG = 2
+W1, W2, W3 = 0, 1, 2
 
 
 def tile_picked_bpclip_none_po_kernel(
@@ -41,52 +47,66 @@ def tile_picked_bpclip_none_po_kernel(
 
     with ExitStack() as ctx:
         keep = ctx.enter_context(tc.tile_pool(name="keep", bufs=1))
-        ring = ctx.enter_context(tc.tile_pool(name="ring", bufs=2))
-        deep = ctx.enter_context(tc.tile_pool(name="deep", bufs=4))
+        diffs = ctx.enter_context(tc.tile_pool(name="diffs", bufs=3))
+        per_block = ctx.enter_context(tc.tile_pool(name="per_block", bufs=4))
         psum = ctx.enter_context(tc.psum_pool(name="psum", bufs=2))
 
         lists = {}
         for name in ("offs", "r1", "r2", "p1", "p2"):
-            lists[name] = keep.tile([P, S // 16], U16, name="list_" + name)
-        x_w = keep.tile([P, T], I32, tag="dealt_s0", align_bytes=64)
+            lists[name] = keep.tile([P, S // GROUP], U16, name="list_" + name)
+        x_w = keep.tile([P, T], I32, tag="x_then_w1_scales", align_bytes=64)
         x_s = keep.tile([P, T], U8, align_bytes=64)
-        raw_w = [keep.tile([P, H], I32, name="raw_w%d" % i, align_bytes=64) for i in range(3)]
-        raw_s = [keep.tile([P, H], U8, name="raw_s%d" % i, align_bytes=64) for i in range(3)]
-        w_w = [keep.tile([P, H], I32, name="w_w%d" % i, align_bytes=64) for i in range(2)]
-        w_s = [keep.tile([P, H], U8, name="w_s%d" % i, tag="dealt_s%d" % i, align_bytes=64) for i in range(2)]
+        raw_w = [keep.tile([P, H], I32, name="raw_w%d" % w, align_bytes=64) for w in (W1, W2, W3)]
+        raw_s = [keep.tile([P, H], U8, name="raw_s%d" % w, align_bytes=64) for w in (W1, W2, W3)]
+        dealt_w = [keep.tile([P, H], I32, name="dealt_w%d" % w, align_bytes=64) for w in (W1, W2)]
+        dealt_s = [
+            keep.tile([P, H], U8, name="dealt_s0", tag="x_then_w1_scales", align_bytes=64),
+            keep.tile([P, H], U8, name="dealt_s1", align_bytes=64),
+        ]
         gain = keep.tile([P, PACK], F32)
         upper = keep.tile([P, PACK], F32)
         lower = keep.tile([P, PACK], F32)
         ident = keep.tile([P, P], F32)
 
-        for q in range(4):
+        for q in range(QUADRANTS):
             load_scale_rows(nc.sync, x_s, x_scales, q)
         nc.sync.dma_start(lists["offs"][:], offs)
         nc.sync.dma_start(out=x_w[:], in_=words_of(x_words))
-        nc.sync.dma_start(out=raw_w[1][:], in_=words_of(w2_words))
-        for q in range(4):
-            load_scale_rows(nc.sync, raw_s[1], w2_scales, q)
+        nc.sync.dma_start(out=raw_w[W2][:], in_=words_of(w2_words))
+        for q in range(QUADRANTS):
+            load_scale_rows(nc.sync, raw_s[W2], w2_scales, q)
         nc.scalar.dma_start(out=gain[:], in_=gn.rearrange("(p t) o -> p (t o)", t=PACK))
-        nc.sync.dma_start(out=raw_w[0][:], in_=words_of(w1_words))
-        for q in range(4):
-            load_scale_rows((nc.scalar, nc.sync, nc.gpsimd, nc.gpsimd)[q], raw_s[0], w1_scales, q)
+        nc.sync.dma_start(out=raw_w[W1][:], in_=words_of(w1_words))
+        for q, queue in enumerate((nc.scalar, nc.sync, nc.gpsimd, nc.gpsimd)):
+            load_scale_rows(queue, raw_s[W1], w1_scales, q)
         nc.sync.dma_start(lists["r1"][:], r1)
         nc.sync.dma_start(lists["r2"][:], r2)
         nc.sync.dma_start(lists["p1"][:], p1)
         nc.sync.dma_start(lists["p2"][:], p2)
-        nc.sync.dma_start(out=raw_w[2][:], in_=words_of(w3_words))
-        for q in range(4):
-            load_scale_rows(nc.sync, raw_s[2], w3_scales, q)
+        nc.sync.dma_start(out=raw_w[W3][:], in_=words_of(w3_words))
+        for q in range(QUADRANTS):
+            load_scale_rows(nc.sync, raw_s[W3], w3_scales, q)
         make_identity(nc, ident[:])
 
-        def deal(i, ts=slice(0, PACK)):
+        def deal(w, planes=slice(0, PACK)):
             nc.vector.tensor_copy(
-                out=w_w[i][:].rearrange("p (t c i) -> p c t i", t=PACK, i=4)[:, :, ts, :],
-                in_=raw_w[i][:].rearrange("p (c i t) -> p c t i", t=PACK, i=4)[:, :, ts, :],
+                out=dealt_w[w][:].rearrange("p (t c i) -> p c t i", t=PACK, i=LINE)[:, :, planes, :],
+                in_=raw_w[w][:].rearrange("p (c i t) -> p c t i", t=PACK, i=LINE)[:, :, planes, :],
             )
             nc.vector.tensor_copy(
-                out=w_s[i][:].rearrange("p (t m) -> p t m", t=PACK)[:, ts, :],
-                in_=raw_s[i][:].rearrange("p (m t) -> p t m", t=PACK)[:, ts, :],
+                out=dealt_s[w][:].rearrange("p (t m) -> p t m", t=PACK)[:, planes, :],
+                in_=raw_s[w][:].rearrange("p (m t) -> p t m", t=PACK)[:, planes, :],
+            )
+
+        def multiply(out, w, t, codes, scales):
+            nc.tensor.matmul_mx(
+                out=out,
+                lhsT=dealt_w[w][:, t * P : (t + 1) * P].bitcast(FP8X4),
+                lhsT_scale=dealt_s[w][:, t * P : (t + 1) * P],
+                rhs=codes.bitcast(FP8X4),
+                rhs_scale=scales,
+                start=True,
+                stop=True,
             )
 
         xq_w = keep.tile([P, S], U32, align_bytes=64)
@@ -95,50 +115,44 @@ def tile_picked_bpclip_none_po_kernel(
         for h in range(2):
             nc.vector.tensor_copy(
                 xq_w[:, h * HALF : (h + 1) * HALF],
-                x_w[:].bitcast(U32).indirect(lists["offs"][:, h * HALF // 16 : (h + 1) * HALF // 16]),
+                x_w[:].bitcast(U32).indirect(lists["offs"][:, h * HALF // GROUP : (h + 1) * HALF // GROUP]),
             )
-            deal(1, slice(0, 2) if h == 0 else slice(2, PACK))
-        deal(0)
+            deal(W2, slice(2 * h, 2 * h + 2))
+        deal(W1)
 
         nc.scalar.activation(out=upper[:], in_=gain[:], func=ACT.Abs, scale=CLIP)
         nc.scalar.activation(out=lower[:], in_=upper[:], func=ACT.Copy, scale=-1.0)
 
+        def first_product(rows, w, t, width):
+            for j0 in range(0, S, width):
+                cols = slice(j0, j0 + width)
+                acc = psum.tile([P, width], F32, name="wide")
+                multiply(acc[:], w, t, xq_w[:, cols], xq_s[:, cols])
+                nc.scalar.activation(out=rows[:, cols], in_=acc[:], func=ACT.Copy, scale=gain[:, t : t + 1])
+
         beliefs, messages = [], []
         for t in range(PACK):
-            cols = slice(t * P, (t + 1) * P)
-            for i, name, into in ((1, "e", messages), (0, "y", beliefs)):
-                rows = keep.tile([P, 2 * S if i == 1 else S], F32, name="%s%d" % (name, t), align_bytes=64)
-                if i == 1:
-                    nc.vector.memset(rows[:, S:], 0.0)
-                width = HALF if not messages else S
-                for j0 in range(0, S, width):
-                    acc = psum.tile([P, width], F32, name="first")
-                    nc.tensor.matmul_mx(
-                        out=acc[:],
-                        lhsT=w_w[i][:, cols].bitcast(FP8X4),
-                        lhsT_scale=w_s[i][:, cols],
-                        rhs=xq_w[:, j0 : j0 + width].bitcast(FP8X4),
-                        rhs_scale=xq_s[:, j0 : j0 + width],
-                        start=True,
-                        stop=True,
-                    )
-                    nc.scalar.activation(
-                        out=rows[:, j0 : j0 + width], in_=acc[:], func=ACT.Copy, scale=gain[:, t : t + 1]
-                    )
-                into.append(rows)
+            messages.append(keep.tile([P, 2 * S], F32, name="e%d" % t, align_bytes=64))
+            nc.vector.memset(messages[t][:, S:], 0.0)
+            first_product(messages[t], W2, t, HALF if t == 0 else S)
+            beliefs.append(keep.tile([P, S], F32, name="y%d" % t, align_bytes=64))
+            first_product(beliefs[t], W1, t, S)
 
         out_words = keep.tile([P, S], I32, align_bytes=64)
         out_scales = keep.tile([P, S], U8, align_bytes=64)
         out_rows = out_0.rearrange("(p t) j -> p t j", t=PACK)
 
         steps = [(j0, n, t) for j0, n in STRETCHES for t in range(PACK)]
-        shared = {"diff0", "diff1"}
+        multiply_at = {PACK - 1 + MULTIPLY_LAG + block: block for block in range(STRETCHES[0][1] // BLOCK)}
+        hand_on_at = {step + HAND_ON_LAG: block for step, block in multiply_at.items()}
+        last_block = S // BLOCK - 1
+        own_bytes = {0, 1} | set(multiply_at)
+        z_tags = {block: "diff%d" % step for step, block in multiply_at.items()}
 
-        def quantiser_input(tag):
-            shared.add(tag)
-            return keep.tile([P, BLOCK * PACK], BF16, name="before_" + tag, tag=tag, align_bytes=64)
-
-        fetched = []
+        fetched, banks, z_tiles, rounded = [], {}, {}, {}
+        last_clipped = keep.tile([P, 2, 2, BLOCK], F32)
+        last_partial = keep.tile([P, 2, BLOCK], F32)
+        z_tiles[last_block] = keep.tile([P, BLOCK * PACK], BF16, name="z_last", align_bytes=64)
 
         def fetch_messages(t):
             got = keep.tile([P, 2, S], F32, name="got%d" % t)
@@ -146,165 +160,156 @@ def tile_picked_bpclip_none_po_kernel(
                 nc.vector.tensor_copy(got[:, c, :], messages[t][:].indirect(lists[name][:]))
             fetched.append(got)
 
+        def difference(out, c, j0, n, t):
+            offsets = lists[("p1", "p2")[c]][:, j0 // GROUP : (j0 + n) // GROUP]
+            nc.vector.tensor_tensor(out, beliefs[t][:].indirect(offsets), fetched[t][:, c, j0 : j0 + n], ALU.subtract)
+
         def subtract(step):
             j0, n, t = steps[step]
-            tag = "diff%d" % step
-            if tag in shared:
-                diff = keep.tile([P, 2, n], F32, name=tag, tag=tag, align_bytes=64)
+            if step in own_bytes:
+                diff = keep.tile([P, 2, n], F32, name="diff%d" % step, tag="diff%d" % step, align_bytes=64)
             else:
-                diff = ring.tile([P, 2, n], F32, name="diff", bufs=3)
-            for c, name in enumerate(("p1", "p2")):
-                at = lists[name][:, j0 // 16 : (j0 + n) // 16]
-                nc.vector.tensor_tensor(
-                    diff[:, c, :], beliefs[t][:].indirect(at), fetched[t][:, c, j0 : j0 + n], ALU.subtract
-                )
+                diff = diffs.tile([P, 2, n], F32, name="diff")
+            for c in range(2):
+                difference(diff[:, c, :], c, j0, n, t)
             return diff
-
-        before_fetch, before_subtract = {}, {}
-        banks = {}
-        last_clipped = keep.tile([P, 2, 2, BLOCK], F32)
-        last_partial = keep.tile([P, 2, BLOCK], F32)
-        last_z = keep.tile([P, BLOCK * PACK], BF16, align_bytes=64)
 
         def clip(out, diff, t):
             nc.vector.tensor_scalar(out, diff, lower[:, t : t + 1], upper[:, t : t + 1], ALU.max, ALU.min)
 
-        def last_pair(waiting):
+        def clip_and_sum(step, diff):
+            j0, n, t = steps[step]
+            blocks = range(j0 // BLOCK, (j0 + n) // BLOCK)
+            clipped = keep.tile([P, 2, n], F32, name="clipped%d" % step)
+            clip(clipped[:], diff[:], t)
+            for block in blocks:
+                if t == 0:
+                    banks[block] = (
+                        psum.tile([P, PACK, P], F32, name="sums"),
+                        psum.tile([P, 2, BLOCK], F32, name="turned"),
+                    )
+                within = slice(block * BLOCK - j0, (block + 1) * BLOCK - j0)
+                terms = (beliefs[t][:, block * BLOCK : (block + 1) * BLOCK], clipped[:, 0, within], clipped[:, 1, within])
+                for index, term in enumerate(terms):
+                    nc.tensor.matmul(
+                        banks[block][0][:, t, :], lhsT=term, rhs=ident[:], is_transpose=True,
+                        start=(index == 0), stop=(index == len(terms) - 1),
+                    )
+            if t % 2 == 0:
+                return
+            for block in blocks:
+                sums, turned = banks[block]
+                pairs = per_block.tile([P, P, 2], BF16, name="pairs", align_bytes=64)
+                nc.scalar.copy(out=pairs[:], in_=sums[:, t - 1 : t + 1, :].rearrange("j e p -> j p e"))
+                nc.tensor.transpose(turned[:, t // 2, :], pairs[:].rearrange("j p e -> j (p e)").bitcast(F32), ident[:])
+                if block == last_block:
+                    z_words = z_tiles[block][:].bitcast(F32).rearrange("p (j u) -> p j u", u=2)
+                    nc.scalar.copy(out=z_words[:, :, 0], in_=turned[:, 0, :])
+                elif t == PACK - 1:
+                    tag = z_tags.get(block, "z%d" % block)
+                    z_tiles[block] = keep.tile([P, BLOCK * PACK], BF16, name="z%d" % block, tag=tag, align_bytes=64)
+                    nc.scalar.copy(
+                        out=z_tiles[block][:].bitcast(F32).rearrange("p (j u) -> p j u", u=2),
+                        in_=turned[:].rearrange("p u j -> p j u"),
+                    )
+
+        def quantise_z(block):
+            z_w = per_block.tile([P, BLOCK], U32, name="z_w", align_bytes=64)
+            z_s = per_block.tile([P, BLOCK], U8, name="z_s", align_bytes=64)
+            nc.vector.quantize_mx(out=z_w[:].bitcast(FP8X4), scales=z_s[:], in_=z_tiles[block][:])
+            return z_w, z_s
+
+        def second_product(block):
+            z_w, z_s = quantise_z(block)
+            acc = psum.tile([P, PACK, BLOCK], F32, name="second")
+            for t in range(PACK):
+                multiply(acc[:, t, :], W3, t, z_w[:], z_s[:])
+            result = per_block.tile([P, PACK, BLOCK], F32, name="result")
+            rounded[block] = per_block.tile([P, BLOCK * PACK], BF16, name="rounded", align_bytes=64)
+            nc.scalar.copy(out=result[:], in_=acc[:])
+            nc.sync.dma_start(out=out_rows[:, :, block * BLOCK : (block + 1) * BLOCK], in_=result[:])
+            nc.scalar.copy(
+                out=rounded[block][:].rearrange("p (j t) -> p j t", t=PACK), in_=acc[:].rearrange("p t j -> p j t")
+            )
+
+        def last_second_product():
+            z_w, z_s = quantise_z(last_block)
+            accs = [psum.tile([P, PACK, BLOCK], F32, name="wide") for half in range(2)]
+            for t in range(PACK):
+                multiply(accs[t // 2][:, t, :], W3, t, z_w[:], z_s[:])
+            result = per_block.tile([P, PACK, BLOCK], F32, name="result")
+            rounded[last_block] = per_block.tile([P, BLOCK * PACK], BF16, name="rounded", align_bytes=64)
+            for half in range(2):
+                planes = slice(2 * half, 2 * half + 2)
+                nc.vector.tensor_copy(out=result[:, planes, :], in_=accs[half][:, planes, :])
+                nc.sync.dma_start(out=out_rows[:, planes, last_block * BLOCK :], in_=result[:, planes, :])
+            nc.vector.tensor_copy(
+                out=rounded[last_block][:].rearrange("p (c i t) -> p c t i", t=PACK, i=LINE),
+                in_=result[:].rearrange("p t (c i) -> p c t i", i=LINE),
+            )
+
+        def quantise_result(block):
+            cols = slice(block * BLOCK, (block + 1) * BLOCK)
+            nc.vector.quantize_mx(
+                out=out_words[:, cols].bitcast(FP8X4), scales=out_scales[:, cols], in_=rounded[block][:]
+            )
+
+        def store_words(first, last):
+            cols = slice(first * BLOCK, (last + 1) * BLOCK)
+            nc.sync.dma_start(out=words_of(out_1)[:, cols], in_=out_words[:, cols])
+
+        def hand_on(block):
+            quantise_result(block)
+            store_words(block, block)
+
+        def last_two_steps(waiting):
             j0, n = STRETCHES[-1]
-            diff = ring.tile([P, 2, 2, n], F32, name="diff", bufs=3)
-
-            def difference(c, e):
-                at = lists[("p1", "p2")[c]][:, j0 // 16 : (j0 + n) // 16]
-                nc.vector.tensor_tensor(
-                    diff[:, c, e, :], beliefs[2 + e][:].indirect(at), fetched[2 + e][:, c, j0 : j0 + n], ALU.subtract
-                )
-
-            difference(0, 0)
-            difference(0, 1)
+            diff = diffs.tile([P, 2, 2, n], F32, name="diff")
+            for e in range(2):
+                difference(diff[:, 0, e, :], 0, j0, n, 2 + e)
             clip_and_sum(len(steps) - 3, waiting)
-            difference(1, 0)
+            difference(diff[:, 1, 0, :], 1, j0, n, 2)
             for e in range(2):
                 clip(last_clipped[:, 0, e, :], diff[:, 0, e, :], 2 + e)
             for e in range(2):
                 nc.vector.tensor_tensor(
                     last_partial[:, e, :], beliefs[2 + e][:, j0 : j0 + n], last_clipped[:, 0, e, :], ALU.add
                 )
-            difference(1, 1)
+            difference(diff[:, 1, 1, :], 1, j0, n, 3)
             for e in range(2):
                 clip(last_clipped[:, 1, e, :], diff[:, 1, e, :], 2 + e)
-            before_fetch[len(steps)]()
+            second_product(last_block - 1)
             nc.vector.tensor_tensor(
-                last_z[:].rearrange("p (c i t) -> p c t i", t=PACK, i=4)[:, :, 2:4, :],
-                last_partial[:].rearrange("p e (c i) -> p c e i", i=4),
-                last_clipped[:, 1, :, :].rearrange("p e (c i) -> p c e i", i=4),
+                z_tiles[last_block][:].rearrange("p (c i t) -> p c t i", t=PACK, i=LINE)[:, :, 2:4, :],
+                last_partial[:].rearrange("p e (c i) -> p c e i", i=LINE),
+                last_clipped[:, 1, :, :].rearrange("p e (c i) -> p c e i", i=LINE),
                 ALU.add,
             )
-            second_product(j0, last_z, len(steps))
 
-        def clip_and_sum(step, diff):
-            j0, n, t = steps[step]
-            last = j0 + n == S
-            clipped = keep.tile([P, 2, n], F32, name="clipped%d" % step)
-            clip(clipped[:], diff[:], t)
-            for b in range(n // BLOCK):
-                lo = b * BLOCK
-                if t == 0:
-                    banks[b] = (psum.tile([P, PACK, P], F32, name="sums"), psum.tile([P, 2, BLOCK], F32, name="turned"))
-                sums, turned = banks[b]
-                terms = (
-                    beliefs[t][:, j0 + lo : j0 + lo + BLOCK],
-                    clipped[:, 0, lo : lo + BLOCK],
-                    clipped[:, 1, lo : lo + BLOCK],
-                )
-                for c, term in enumerate(terms):
-                    nc.tensor.matmul(
-                        sums[:, t, :], lhsT=term, rhs=ident[:], is_transpose=True,
-                        start=(c == 0), stop=(c == len(terms) - 1),
-                    )
-            if t % 2 == 0:
-                return
-            for b in range(n // BLOCK):
-                sums, turned = banks[b]
-                pairs = deep.tile([P, P, 2], BF16, name="pairs", align_bytes=64)
-                nc.scalar.copy(out=pairs[:], in_=sums[:, t - 1 : t + 1, :].rearrange("j e p -> j p e"))
-                nc.tensor.transpose(turned[:, t // 2, :], pairs[:].rearrange("j p e -> j (p e)").bitcast(F32), ident[:])
-                if last:
-                    nc.scalar.copy(
-                        out=last_z[:].bitcast(F32).rearrange("p (j u) -> p j u", u=2)[:, :, 0], in_=turned[:, 0, :]
-                    )
-                elif t == PACK - 1:
-                    at = step + 4 + b + (step > PACK)
-                    z_in = quantiser_input("diff%d" % at)
-                    nc.scalar.copy(
-                        out=z_in[:].bitcast(F32).rearrange("p (j u) -> p j u", u=2),
-                        in_=turned[:].rearrange("p u j -> p j u"),
-                    )
-                    before_fetch[at] = lambda j=j0 + b * BLOCK, z_in=z_in, at=at: second_product(j, z_in, at)
-
-        def second_product(j0, z_in, step):
-            cols = slice(j0, j0 + BLOCK)
-            z_w = deep.tile([P, BLOCK], U32, name="z_w", align_bytes=64)
-            z_s = deep.tile([P, BLOCK], U8, name="z_s", align_bytes=64)
-            nc.vector.quantize_mx(out=z_w[:].bitcast(FP8X4), scales=z_s[:], in_=z_in[:])
-            last = j0 + BLOCK == S
-            accs = [psum.tile([P, PACK, BLOCK], F32, name="first" if last else "second") for half in range(2 if last else 1)]
-            for t in range(PACK):
-                nc.tensor.matmul_mx(
-                    out=accs[t // 2 if last else 0][:, t, :],
-                    lhsT=w_w[2][:, t * P : (t + 1) * P].bitcast(FP8X4),
-                    lhsT_scale=w_s[2][:, t * P : (t + 1) * P],
-                    rhs=z_w[:].bitcast(FP8X4),
-                    rhs_scale=z_s[:],
-                    start=True,
-                    stop=True,
-                )
-            result = deep.tile([P, PACK, BLOCK], F32, name="result")
-            rounded = deep.tile([P, BLOCK * PACK], BF16, name="rounded", align_bytes=64)
-            if not last:
-                nc.scalar.copy(out=result[:], in_=accs[0][:])
-                nc.sync.dma_start(out=out_rows[:, :, cols], in_=result[:])
-                nc.scalar.copy(
-                    out=rounded[:].rearrange("p (j t) -> p j t", t=PACK), in_=accs[0][:].rearrange("p t j -> p j t")
-                )
-                before_subtract[step + 2] = lambda: hand_on(cols, rounded)
-            else:
-                nc.scalar.copy(out=result[:, 0:2, :], in_=accs[0][:, 0:2, :])
-                nc.scalar.dma_start(out=out_rows[:, 0:2, cols], in_=result[:, 0:2, :])
-                nc.vector.tensor_copy(out=result[:, 2:4, :], in_=accs[1][:, 2:4, :])
-                nc.sync.dma_start(out=out_rows[:, 2:4, cols], in_=result[:, 2:4, :])
-                before_subtract[len(steps) + 2]()
-                nc.vector.tensor_copy(
-                    out=rounded[:].rearrange("p (c i t) -> p c t i", t=PACK, i=4),
-                    in_=result[:].rearrange("p t (c i) -> p c t i", i=4),
-                )
-                hand_on(cols, rounded)
-
-        def hand_on(cols, rounded):
-            nc.vector.quantize_mx(out=out_words[:, cols].bitcast(FP8X4), scales=out_scales[:, cols], in_=rounded[:])
-            nc.sync.dma_start(out=words_of(out_1)[:, cols], in_=out_words[:, cols])
-
-        def deal_w3():
-            w_w.append(keep.tile([P, H], I32, name="w_w2", tag="diff0", align_bytes=64))
-            w_s.append(keep.tile([P, H], U8, name="w_s2", tag="diff1", align_bytes=64))
-            deal(2)
-
-        before_subtract[3] = deal_w3
         waiting = None
         for step in range(len(steps) - 2):
             if step < PACK:
                 fetch_messages(step)
-            if step in before_fetch:
-                before_fetch[step]()
-            if step in before_subtract:
-                before_subtract[step]()
+            if step in multiply_at:
+                second_product(multiply_at[step])
+            if step in hand_on_at:
+                hand_on(hand_on_at[step])
+            if step == PACK - 1:
+                dealt_w.append(keep.tile([P, N], I32, name="dealt_w2", tag="diff0", align_bytes=64))
+                dealt_s.append(keep.tile([P, N], U8, name="dealt_s2", tag="diff1", align_bytes=64))
+                deal(W3)
             diff = subtract(step)
             if waiting is not None:
                 clip_and_sum(step - 1, waiting)
             waiting = diff
-        before_subtract[len(steps) - 2]()
-        last_pair(waiting)
+        hand_on(hand_on_at[len(steps) - 2])
+        last_two_steps(waiting)
+        last_second_product()
+        quantise_result(last_block - 1)
+        quantise_result(last_block)
+        store_words(last_block - 1, last_block)
 
-        for q in range(4):
+        for q in range(QUADRANTS):
             (nc.sync if q % 2 == 0 else nc.scalar).dma_start(
                 out=out_2[0, 4 * q : 4 * q + 4, :].bitcast(I32),
                 in_=out_scales[32 * q : 32 * q + 4, :].bitcast(I32),

from contextlib import ExitStack

import concourse.mybir as mybir
from concourse.masks import make_identity

K, T, S, N, H = 512, 2048, 512, 512, 512
FLOPS = 2 * S * (2 * K * H + H * N)

F32 = mybir.dt.float32
BF16 = mybir.dt.bfloat16
I32 = mybir.dt.int32
U32 = mybir.dt.uint32
U16 = mybir.dt.uint16
U8 = mybir.dt.uint8
FP8X4 = mybir.dt.float8_e4m3fn_x4
ALU = mybir.AluOpType
ACT = mybir.ActivationFunctionType

P = 128
PACK = 4
QUADRANTS = 4
GROUP = 16
LINE = 4
CLIP = 0.75
HALF = S // 2
BLOCK = 128
STRETCHES = ((0, 2 * BLOCK), (2 * BLOCK, BLOCK), (3 * BLOCK, BLOCK))
MULTIPLY_LAG = 4
HAND_ON_LAG = 2
W1, W2, W3 = 0, 1, 2


def tile_picked_bpclip_none_po_kernel(
    tc, x_words, x_scales, w1_words, w1_scales, w2_words, w2_scales, gn, w3_words, w3_scales,
    offs, p1, r1, p2, r2, out_0, out_1, out_2,
):
    nc = tc.nc

    def words_of(dram):
        return dram[0].rearrange("p n t -> p (n t)").bitcast(I32)

    def load_scale_rows(queue, tile, dram, quadrant):
        queue.dma_start(
            out=tile[32 * quadrant : 32 * quadrant + 32, :].bitcast(I32),
            in_=dram[0, 4 * quadrant : 4 * quadrant + 4, :].bitcast(I32).partition_broadcast(8),
        )

    with ExitStack() as ctx:
        keep = ctx.enter_context(tc.tile_pool(name="keep", bufs=1))
        diffs = ctx.enter_context(tc.tile_pool(name="diffs", bufs=3))
        per_block = ctx.enter_context(tc.tile_pool(name="per_block", bufs=4))
        psum = ctx.enter_context(tc.psum_pool(name="psum", bufs=2))

        lists = {}
        for name in ("offs", "r1", "r2", "p1", "p2"):
            lists[name] = keep.tile([P, S // GROUP], U16, name="list_" + name)
        x_w = keep.tile([P, T], I32, tag="x_then_w1_scales", align_bytes=64)
        x_s = keep.tile([P, T], U8, align_bytes=64)
        raw_w = [keep.tile([P, H], I32, name="raw_w%d" % w, align_bytes=64) for w in (W1, W2, W3)]
        raw_s = [keep.tile([P, H], U8, name="raw_s%d" % w, align_bytes=64) for w in (W1, W2, W3)]
        dealt_w = [keep.tile([P, H], I32, name="dealt_w%d" % w, align_bytes=64) for w in (W1, W2)]
        dealt_s = [
            keep.tile([P, H], U8, name="dealt_s0", tag="x_then_w1_scales", align_bytes=64),
            keep.tile([P, H], U8, name="dealt_s1", align_bytes=64),
        ]
        gain = keep.tile([P, PACK], F32)
        upper = keep.tile([P, PACK], F32)
        lower = keep.tile([P, PACK], F32)
        ident = keep.tile([P, P], F32)

        for q in range(QUADRANTS):
            load_scale_rows(nc.sync, x_s, x_scales, q)
        nc.sync.dma_start(lists["offs"][:], offs)
        nc.sync.dma_start(out=x_w[:], in_=words_of(x_words))
        nc.sync.dma_start(out=raw_w[W2][:], in_=words_of(w2_words))
        for q in range(QUADRANTS):
            load_scale_rows(nc.sync, raw_s[W2], w2_scales, q)
        nc.scalar.dma_start(out=gain[:], in_=gn.rearrange("(p t) o -> p (t o)", t=PACK))
        nc.sync.dma_start(out=raw_w[W1][:], in_=words_of(w1_words))
        for q, queue in enumerate((nc.scalar, nc.sync, nc.gpsimd, nc.gpsimd)):
            load_scale_rows(queue, raw_s[W1], w1_scales, q)
        nc.sync.dma_start(lists["r1"][:], r1)
        nc.sync.dma_start(lists["r2"][:], r2)
        nc.sync.dma_start(lists["p1"][:], p1)
        nc.sync.dma_start(lists["p2"][:], p2)
        nc.sync.dma_start(out=raw_w[W3][:], in_=words_of(w3_words))
        for q in range(QUADRANTS):
            load_scale_rows(nc.sync, raw_s[W3], w3_scales, q)
        make_identity(nc, ident[:])

        def deal(w, planes=slice(0, PACK)):
            nc.vector.tensor_copy(
                out=dealt_w[w][:].rearrange("p (t c i) -> p c t i", t=PACK, i=LINE)[:, :, planes, :],
                in_=raw_w[w][:].rearrange("p (c i t) -> p c t i", t=PACK, i=LINE)[:, :, planes, :],
            )
            nc.vector.tensor_copy(
                out=dealt_s[w][:].rearrange("p (t m) -> p t m", t=PACK)[:, planes, :],
                in_=raw_s[w][:].rearrange("p (m t) -> p t m", t=PACK)[:, planes, :],
            )

        def multiply(out, w, t, codes, scales):
            nc.tensor.matmul_mx(
                out=out,
                lhsT=dealt_w[w][:, t * P : (t + 1) * P].bitcast(FP8X4),
                lhsT_scale=dealt_s[w][:, t * P : (t + 1) * P],
                rhs=codes.bitcast(FP8X4),
                rhs_scale=scales,
                start=True,
                stop=True,
            )

        xq_w = keep.tile([P, S], U32, align_bytes=64)
        xq_s = keep.tile([P, S], U8, align_bytes=64)
        nc.vector.tensor_copy(xq_s[:], x_s[:].indirect(lists["offs"][:]))
        for h in range(2):
            nc.vector.tensor_copy(
                xq_w[:, h * HALF : (h + 1) * HALF],
                x_w[:].bitcast(U32).indirect(lists["offs"][:, h * HALF // GROUP : (h + 1) * HALF // GROUP]),
            )
            deal(W2, slice(2 * h, 2 * h + 2))
        deal(W1)

        nc.scalar.activation(out=upper[:], in_=gain[:], func=ACT.Abs, scale=CLIP)
        nc.scalar.activation(out=lower[:], in_=upper[:], func=ACT.Copy, scale=-1.0)

        def first_product(rows, w, t, width):
            for j0 in range(0, S, width):
                cols = slice(j0, j0 + width)
                acc = psum.tile([P, width], F32, name="wide")
                multiply(acc[:], w, t, xq_w[:, cols], xq_s[:, cols])
                nc.scalar.activation(out=rows[:, cols], in_=acc[:], func=ACT.Copy, scale=gain[:, t : t + 1])

        beliefs, messages = [], []
        for t in range(PACK):
            messages.append(keep.tile([P, 2 * S], F32, name="e%d" % t, align_bytes=64))
            nc.vector.memset(messages[t][:, S:], 0.0)
            first_product(messages[t], W2, t, HALF if t == 0 else S)
            beliefs.append(keep.tile([P, S], F32, name="y%d" % t, align_bytes=64))
            first_product(beliefs[t], W1, t, S)

        out_words = keep.tile([P, S], I32, align_bytes=64)
        out_scales = keep.tile([P, S], U8, align_bytes=64)
        out_rows = out_0.rearrange("(p t) j -> p t j", t=PACK)

        steps = [(j0, n, t) for j0, n in STRETCHES for t in range(PACK)]
        multiply_at = {PACK - 1 + MULTIPLY_LAG + block: block for block in range(STRETCHES[0][1] // BLOCK)}
        hand_on_at = {step + HAND_ON_LAG: block for step, block in multiply_at.items()}
        last_block = S // BLOCK - 1
        own_bytes = {0, 1} | set(multiply_at)
        z_tags = {block: "diff%d" % step for step, block in multiply_at.items()}

        fetched, banks, z_tiles, rounded = [], {}, {}, {}
        last_clipped = keep.tile([P, 2, 2, BLOCK], F32)
        last_partial = keep.tile([P, 2, BLOCK], F32)
        z_tiles[last_block] = keep.tile([P, BLOCK * PACK], BF16, name="z_last", align_bytes=64)

        def fetch_messages(t):
            got = keep.tile([P, 2, S], F32, name="got%d" % t)
            for c, name in enumerate(("r1", "r2")):
                nc.vector.tensor_copy(got[:, c, :], messages[t][:].indirect(lists[name][:]))
            fetched.append(got)

        def difference(out, c, j0, n, t):
            offsets = lists[("p1", "p2")[c]][:, j0 // GROUP : (j0 + n) // GROUP]
            nc.vector.tensor_tensor(out, beliefs[t][:].indirect(offsets), fetched[t][:, c, j0 : j0 + n], ALU.subtract)

        def subtract(step):
            j0, n, t = steps[step]
            if step in own_bytes:
                diff = keep.tile([P, 2, n], F32, name="diff%d" % step, tag="diff%d" % step, align_bytes=64)
            else:
                diff = diffs.tile([P, 2, n], F32, name="diff")
            for c in range(2):
                difference(diff[:, c, :], c, j0, n, t)
            return diff

        def clip(out, diff, t):
            nc.vector.tensor_scalar(out, diff, lower[:, t : t + 1], upper[:, t : t + 1], ALU.max, ALU.min)

        def clip_and_sum(step, diff):
            j0, n, t = steps[step]
            blocks = range(j0 // BLOCK, (j0 + n) // BLOCK)
            clipped = keep.tile([P, 2, n], F32, name="clipped%d" % step)
            clip(clipped[:], diff[:], t)
            for block in blocks:
                if t == 0:
                    banks[block] = (
                        psum.tile([P, PACK, P], F32, name="sums"),
                        psum.tile([P, 2, BLOCK], F32, name="turned"),
                    )
                within = slice(block * BLOCK - j0, (block + 1) * BLOCK - j0)
                terms = (beliefs[t][:, block * BLOCK : (block + 1) * BLOCK], clipped[:, 0, within], clipped[:, 1, within])
                for index, term in enumerate(terms):
                    nc.tensor.matmul(
                        banks[block][0][:, t, :], lhsT=term, rhs=ident[:], is_transpose=True,
                        start=(index == 0), stop=(index == len(terms) - 1),
                    )
            if t % 2 == 0:
                return
            for block in blocks:
                sums, turned = banks[block]
                pairs = per_block.tile([P, P, 2], BF16, name="pairs", align_bytes=64)
                nc.scalar.copy(out=pairs[:], in_=sums[:, t - 1 : t + 1, :].rearrange("j e p -> j p e"))
                nc.tensor.transpose(turned[:, t // 2, :], pairs[:].rearrange("j p e -> j (p e)").bitcast(F32), ident[:])
                if block == last_block:
                    z_words = z_tiles[block][:].bitcast(F32).rearrange("p (j u) -> p j u", u=2)
                    nc.scalar.copy(out=z_words[:, :, 0], in_=turned[:, 0, :])
                elif t == PACK - 1:
                    tag = z_tags.get(block, "z%d" % block)
                    z_tiles[block] = keep.tile([P, BLOCK * PACK], BF16, name="z%d" % block, tag=tag, align_bytes=64)
                    nc.scalar.copy(
                        out=z_tiles[block][:].bitcast(F32).rearrange("p (j u) -> p j u", u=2),
                        in_=turned[:].rearrange("p u j -> p j u"),
                    )

        def quantise_z(block):
            z_w = per_block.tile([P, BLOCK], U32, name="z_w", align_bytes=64)
            z_s = per_block.tile([P, BLOCK], U8, name="z_s", align_bytes=64)
            nc.vector.quantize_mx(out=z_w[:].bitcast(FP8X4), scales=z_s[:], in_=z_tiles[block][:])
            return z_w, z_s

        def second_product(block):
            z_w, z_s = quantise_z(block)
            acc = psum.tile([P, PACK, BLOCK], F32, name="second")
            for t in range(PACK):
                multiply(acc[:, t, :], W3, t, z_w[:], z_s[:])
            result = per_block.tile([P, PACK, BLOCK], F32, name="result")
            rounded[block] = per_block.tile([P, BLOCK * PACK], BF16, name="rounded", align_bytes=64)
            nc.scalar.copy(out=result[:], in_=acc[:])
            nc.sync.dma_start(out=out_rows[:, :, block * BLOCK : (block + 1) * BLOCK], in_=result[:])
            nc.scalar.copy(
                out=rounded[block][:].rearrange("p (j t) -> p j t", t=PACK), in_=acc[:].rearrange("p t j -> p j t")
            )

        def last_second_product():
            z_w, z_s = quantise_z(last_block)
            accs = [psum.tile([P, PACK, BLOCK], F32, name="wide") for half in range(2)]
            for t in range(PACK):
                multiply(accs[t // 2][:, t, :], W3, t, z_w[:], z_s[:])
            result = per_block.tile([P, PACK, BLOCK], F32, name="result")
            rounded[last_block] = per_block.tile([P, BLOCK * PACK], BF16, name="rounded", align_bytes=64)
            for half in range(2):
                planes = slice(2 * half, 2 * half + 2)
                nc.vector.tensor_copy(out=result[:, planes, :], in_=accs[half][:, planes, :])
                nc.sync.dma_start(out=out_rows[:, planes, last_block * BLOCK :], in_=result[:, planes, :])
            nc.vector.tensor_copy(
                out=rounded[last_block][:].rearrange("p (c i t) -> p c t i", t=PACK, i=LINE),
                in_=result[:].rearrange("p t (c i) -> p c t i", i=LINE),
            )

        def quantise_result(block):
            cols = slice(block * BLOCK, (block + 1) * BLOCK)
            nc.vector.quantize_mx(
                out=out_words[:, cols].bitcast(FP8X4), scales=out_scales[:, cols], in_=rounded[block][:]
            )

        def store_words(first, last):
            cols = slice(first * BLOCK, (last + 1) * BLOCK)
            nc.sync.dma_start(out=words_of(out_1)[:, cols], in_=out_words[:, cols])

        def hand_on(block):
            quantise_result(block)
            store_words(block, block)

        def last_two_steps(waiting):
            j0, n = STRETCHES[-1]
            diff = diffs.tile([P, 2, 2, n], F32, name="diff")
            for e in range(2):
                difference(diff[:, 0, e, :], 0, j0, n, 2 + e)
            clip_and_sum(len(steps) - 3, waiting)
            difference(diff[:, 1, 0, :], 1, j0, n, 2)
            for e in range(2):
                clip(last_clipped[:, 0, e, :], diff[:, 0, e, :], 2 + e)
            for e in range(2):
                nc.vector.tensor_tensor(
                    last_partial[:, e, :], beliefs[2 + e][:, j0 : j0 + n], last_clipped[:, 0, e, :], ALU.add
                )
            difference(diff[:, 1, 1, :], 1, j0, n, 3)
            for e in range(2):
                clip(last_clipped[:, 1, e, :], diff[:, 1, e, :], 2 + e)
            second_product(last_block - 1)
            nc.vector.tensor_tensor(
                z_tiles[last_block][:].rearrange("p (c i t) -> p c t i", t=PACK, i=LINE)[:, :, 2:4, :],
                last_partial[:].rearrange("p e (c i) -> p c e i", i=LINE),
                last_clipped[:, 1, :, :].rearrange("p e (c i) -> p c e i", i=LINE),
                ALU.add,
            )

        waiting = None
        for step in range(len(steps) - 2):
            if step < PACK:
                fetch_messages(step)
            if step in multiply_at:
                second_product(multiply_at[step])
            if step in hand_on_at:
                hand_on(hand_on_at[step])
            if step == PACK - 1:
                dealt_w.append(keep.tile([P, N], I32, name="dealt_w2", tag="diff0", align_bytes=64))
                dealt_s.append(keep.tile([P, N], U8, name="dealt_s2", tag="diff1", align_bytes=64))
                deal(W3)
            diff = subtract(step)
            if waiting is not None:
                clip_and_sum(step - 1, waiting)
            waiting = diff
        hand_on(hand_on_at[len(steps) - 2])
        last_two_steps(waiting)
        last_second_product()
        quantise_result(last_block - 1)
        quantise_result(last_block)
        store_words(last_block - 1, last_block)

        for q in range(QUADRANTS):
            (nc.sync if q % 2 == 0 else nc.scalar).dma_start(
                out=out_2[0, 4 * q : 4 * q + 4, :].bitcast(I32),
                in_=out_scales[32 * q : 32 * q + 4, :].bitcast(I32),
            )
